import numpy as np, ml_dtypes
CORES = [8,136,40,168]
N = 4
import mx_ref
NC = 256
BF = ml_dtypes.bfloat16
def setup_inputs(rng):
    def f(*shape):
        return mx_ref.flush((rng.standard_normal(shape, dtype=np.float32) * np.exp2(rng.integers(-2, 3, shape[:-1] + (1,)))).astype(BF))
    return {"x": f(N, 128, 512), "rt": f(N, 128, 512), "w": f(N, 128, 4 * NC)}
def setup_inputs_blocks(rng):
    d = setup_inputs(rng)
    for k in ("x", "rt", "w"): d[k] = mx_ref.spread(d[k], rng, 1)
    return d
def setup_inputs_wide(rng):
    d = setup_inputs(rng)
    for k in ("x", "rt", "w"): d[k] = mx_ref.flush((d[k].astype(np.float32) * np.exp2(rng.integers(-6, 7, (N, 1, 1))).astype(np.float32)).astype(BF))
    return d
def setup_inputs_near(rng):
    d = setup_inputs(rng); v = d["rt"].astype(np.float32).reshape(N, 128, -1, 4)
    d["rt"] = mx_ref.flush((v[:, :, :1] + v / 64).reshape(d["rt"].shape).astype(BF))
    return d
def setup_inputs_twins(rng):
    d = setup_inputs(rng); v = d["rt"].reshape(N, 128, -1, 4).copy()
    v[:, :, 1] = v[:, :, 0]
    d["rt"] = v.reshape(d["rt"].shape)
    return d
def reference(x, rt, w):
    W = [mx_ref.quantize(w[e]) for e in range(N)]
    y = np.zeros((N, 128, NC), np.float32)
    for j in range(N):
        X = mx_ref.quantize(x[j])
        lg = mx_ref.matmul(X, mx_ref.quantize(rt[j]))[:, :N]
        m = lg.max(axis=1, keepdims=True); m2 = np.where(lg < m, lg, -np.inf).max(axis=1, keepdims=True)
        for e in range(N):
            y[j] = y[j] + (lg[:, e:e + 1] >= m2) * (mx_ref.matmul(X, W[e]) * lg[:, e:e + 1])
    return {"y": y}

@@ -1,0 +1,127 @@
+from concourse.bass import DstId, RemoteDMATransfer
+from concourse.mybir import dt, AluOpType, AxisListType, ActivationFunctionType
+
+N = 4
+NC = 256
+H = NC // 2
+BIG = -1e29
+
+SCRATCH = {
+    "wt": ("sbuf", [128, 4 * NC], "bfloat16"),
+    "xt": ("sbuf", [128, 512], "bfloat16"),
+    "rtt": ("sbuf", [128, 512], "bfloat16"),
+    "xq": ("sbuf", [128, 128], "float8_e4m3fn_x4"),
+    "xs": ("sbuf", [128, 128], "uint8"),
+    "rq": ("sbuf", [128, 128], "float8_e4m3fn_x4"),
+    "rs": ("sbuf", [128, 128], "uint8"),
+    "m": ("sbuf", [128, 4], "float32"),
+    "pen": ("sbuf", [128, 4], "float32"),
+    "low": ("sbuf", [128, 4], "float32"),
+    "m2": ("sbuf", [128, 4], "float32"),
+    "take": ("sbuf", [128, 4], "float32"),
+    "gate": ("sbuf", [128, 4], "float32"),
+    "plog": ("psum", [128, 512], "float32"),
+    "pown": ("psum", [128, 512], "float32"),
+}
+SEMAPHORES = ["lw", "lx", "lr", "qw", "qx", "qr", "plog", "pown", "v", "gate", "sent", "stored"]
+for _e in range(N):
+    SCRATCH["wq%d" % _e] = ("sbuf", [128, NC], "float8_e4m3fn_x4")
+    SCRATCH["ws%d" % _e] = ("sbuf", [128, NC], "uint8")
+    SCRATCH["s%d" % _e] = ("sbuf", [128, NC], "float32")
+    SCRATCH["acc%d" % _e] = ("sbuf", [128, NC], "float32")
+    SEMAPHORES += ["arr%d" % _e]
+    for _h in range(2):
+        SEMAPHORES += ["p%d%d" % (_e, _h), "s%d%d" % (_e, _h)]
+        if _e:
+            SCRATCH["p%d%d" % (_e, _h)] = ("psum", [128, 512], "float32")
+
+
+def rank_program(g, core, T, topo):
+    me = T.rank_of(core)
+    if me is None:
+        return
+    sem = T.sem
+    peers = [(me + k) % N for k in range(1, N)]
+    froms = [(me - k) % N for k in range(1, N)]
+
+    g.sync.dma_start(T.wt[:], T.w[:]).then_inc(sem.lw, 16)
+    g.sync.dma_start(T.xt[:], T.x[:]).then_inc(sem.lx, 16)
+    g.sync.dma_start(T.rtt[:], T.rt[:]).then_inc(sem.lr, 16)
+
+    wq, ws = T["wq%d" % me], T["ws%d" % me]
+    g.vector.wait_ge(sem.lw, 16)
+    g.vector.quantize_mx(wq[:], ws[:], T.wt[:]).then_inc(sem.qw, 1)
+    g.vector.wait_ge(sem.lx, 16)
+    g.vector.quantize_mx(T.xq[:], T.xs[:], T.xt[:]).then_inc(sem.qx, 1)
+    g.vector.wait_ge(sem.lr, 16)
+    g.vector.quantize_mx(T.rq[:], T.rs[:], T.rtt[:]).then_inc(sem.qr, 1)
+
+    mask, ids = None, []
+    for r in peers:
+        d = T.cores[r]
+        one = topo.mask(core, d)
+        mask = one if mask is None else mask & one
+        rid, pid = topo.addr(d, core)
+        ids.append(DstId(rid=rid, pnc=pid))
+    engines = bin(mask).count("1")
+    arr = sem["arr%d" % me]
+    g.wait_ge(sem.qw, 1)
+    for view in (lambda: ws[:], lambda: wq[:].bitcast(dt.uint8)):
+        g.remote_dma_fused([RemoteDMATransfer(dst_ids=ids, dma_engine_mask=mask, remote_sem=arr,
+                                              srcs=[view()], dsts=[view() for _ in peers])], local_sem=sem.sent)
+    g.wait_ge(sem.sent, 2 * engines)
+
+    g.tensor.wait_ge(sem.qx, 1)
+    g.tensor.wait_ge(sem.qr, 1)
+    g.tensor.matmul_mx(T.plog[:, 0:128], T.xq[:], T.xs[:], T.rq[:], T.rs[:], True, True).then_inc(sem.plog, 1)
+    g.tensor.wait_ge(sem.qw, 1)
+    g.tensor.matmul_mx(T.pown[:, 0:NC], T.xq[:], T.xs[:], wq[:], ws[:], True, True).then_inc(sem.pown, 1)
+    for k, e in enumerate(froms, 1):
+        g.tensor.wait_ge(sem["arr%d" % e], 2 * engines)
+        for h in range(2):
+            a, b = h * H, h * H + H
+            g.tensor.matmul_mx(T["p%d%d" % (k, h)][:, 0:H], T.xq[:], T.xs[:], T["wq%d" % e][:, a:b], T["ws%d" % e][:, a:b],
+                               True, True).then_inc(sem["p%d%d" % (k, h)], 1)
+
+    V = g.vector
+    n = [0]
+
+    def step(call):
+        call.then_inc(sem.v, 1)
+        n[0] += 1
+        V.wait_ge(sem.v, n[0])
+
+    L = T.plog[:, 0:N]
+    V.wait_ge(sem.plog, 1)
+    step(V.tensor_reduce(T.m[:, 0:1], L, AxisListType.X, AluOpType.max))
+    step(V.tensor_scalar(T.pen[:], L, T.m[:, 0:1], BIG, AluOpType.is_ge, AluOpType.mult))
+    step(V.tensor_tensor(T.low[:], L, T.pen[:], AluOpType.add))
+    step(V.tensor_reduce(T.m2[:, 0:1], T.low[:], AxisListType.X, AluOpType.max))
+    step(V.tensor_scalar(T.take[:], L, T.m2[:, 0:1], None, AluOpType.is_ge))
+    V.tensor_tensor(T.gate[:], L, T.take[:], AluOpType.mult).then_inc(sem.gate, 1)
+
+    S = g.scalar
+    S.wait_ge(sem.gate, 1)
+    S.wait_ge(sem.pown, 1)
+    S.activation(T.s0[:], T.pown[:, 0:NC], ActivationFunctionType.Copy, scale=T.gate[:, me:me + 1]).then_inc(sem.s00, 1)
+    for k, e in enumerate(froms, 1):
+        for h in range(2):
+            a, b = h * H, h * H + H
+            S.wait_ge(sem["p%d%d" % (k, h)], 1)
+            S.activation(T["s%d" % k][:, a:b], T["p%d%d" % (k, h)][:, 0:H], ActivationFunctionType.Copy,
+                         scale=T.gate[:, e:e + 1]).then_inc(sem["s%d%d" % (k, h)], 1)
+
+    V.wait_ge(sem.s00, 1)
+    for k in range(1, N):
+        prev = T.s0 if k == 1 else T["acc%d" % (k - 1)]
+        for h in range(2):
+            a, b = h * H, h * H + H
+            V.wait_ge(sem["s%d%d" % (k, h)], 1)
+            if k > 1:
+                V.wait_ge(sem["p0%d" % h], k - 1)
+            V.tensor_tensor(T["acc%d" % k][:, a:b], prev[:, a:b], T["s%d" % k][:, a:b], AluOpType.add).then_inc(sem["p0%d" % h], 1)
+
+    g.sync.wait_ge(sem.p00, N - 1)
+    g.sync.wait_ge(sem.p01, N - 1)
+    g.sync.dma_start(T.y[:], T["acc%d" % (N - 1)][:]).then_inc(sem.stored, 16)
+    g.sync.wait_ge(sem.stored, 16)

@@ -6,6 +6,8 @@ NC = 256
 H = NC // 2
 BIG = -1e29
 
+TAIL = [(1, 0), (3, 0), (1, 1), (2, 1), (2, 0), (3, 1)]
+
 SCRATCH = {
     "wt": ("sbuf", [128, 4 * NC], "bfloat16"),
     "xt": ("sbuf", [128, 512], "bfloat16"),
@@ -23,65 +25,109 @@ SCRATCH = {
     "plog": ("psum", [128, 512], "float32"),
     "pown": ("psum", [128, 512], "float32"),
 }
-SEMAPHORES = ["lw", "lx", "lr", "qw", "qx", "qr", "plog", "pown", "v", "gate", "sent", "stored"]
+SEMAPHORES = ["lw0", "lw1", "lx", "lr", "qw0", "qw1", "qx", "qr", "plog", "pown", "v", "gate", "sent", "stored", "sown", "relay",
+              "acc0", "acc1"]
 for _e in range(N):
     SCRATCH["wq%d" % _e] = ("sbuf", [128, NC], "float8_e4m3fn_x4")
     SCRATCH["ws%d" % _e] = ("sbuf", [128, NC], "uint8")
     SCRATCH["s%d" % _e] = ("sbuf", [128, NC], "float32")
     SCRATCH["acc%d" % _e] = ("sbuf", [128, NC], "float32")
-    SEMAPHORES += ["arr%d" % _e]
+    SEMAPHORES += ["arr%d%s" % (_e, _p) for _p in ("first", "second", "relayed")]
     for _h in range(2):
-        SEMAPHORES += ["p%d%d" % (_e, _h), "s%d%d" % (_e, _h)]
         if _e:
             SCRATCH["p%d%d" % (_e, _h)] = ("psum", [128, 512], "float32")
+            SEMAPHORES += ["p%d%d" % (_e, _h), "s%d%d" % (_e, _h)]
+
+
+def count(mask):
+    return bin(mask).count("1")
+
+
+def helper_of(cores, r, topo):
+    a, d, c = cores[r], cores[(r + 2) % N], 0
+    while not (topo.host(c) == topo.host(a) and topo.chip(c) == topo.chip(a) and topo.die(c) != topo.die(a) and topo.may_write(c, d)):
+        c += 1
+    return c
+
+
+def relay_program(g, core, T, topo, r):
+    a, d = T.cores[r], T.cores[(r + 2) % N]
+    piece = lambda: T["wq%d" % r][:, 0:H].bitcast(dt.uint8)
+    mask = topo.mask(core, d)
+    rid, pid = topo.addr(d, core)
+    g.wait_ge(T.sem.relay, count(topo.mask(a, core) & ~topo.mask(a, d)))
+    g.remote_dma(piece(), piece(), T.sem["arr%drelayed" % r], T.sem.sent, pid, rid, mask)
+    g.wait_ge(T.sem.sent, count(mask))
 
 
 def rank_program(g, core, T, topo):
     me = T.rank_of(core)
+    helpers = [helper_of(T.cores, r, topo) for r in range(N)]
     if me is None:
+        if core in helpers:
+            relay_program(g, core, T, topo, helpers.index(core))
         return
     sem = T.sem
-    peers = [(me + k) % N for k in range(1, N)]
-    froms = [(me - k) % N for k in range(1, N)]
+    halves = [(0, H), (H, NC)]
 
-    g.sync.dma_start(T.wt[:], T.w[:]).then_inc(sem.lw, 16)
+    for h, (a, b) in enumerate(halves):
+        g.sync.dma_start(T.wt[:, 4 * a:4 * b], T.w[:, 4 * a:4 * b]).then_inc(sem["lw%d" % h], 16)
     g.sync.dma_start(T.xt[:], T.x[:]).then_inc(sem.lx, 16)
     g.sync.dma_start(T.rtt[:], T.rt[:]).then_inc(sem.lr, 16)
 
     wq, ws = T["wq%d" % me], T["ws%d" % me]
-    g.vector.wait_ge(sem.lw, 16)
-    g.vector.quantize_mx(wq[:], ws[:], T.wt[:]).then_inc(sem.qw, 1)
+    for h, (a, b) in enumerate(halves):
+        g.vector.wait_ge(sem["lw%d" % h], 16)
+        g.vector.quantize_mx(wq[:, a:b], ws[:, a:b], T.wt[:, 4 * a:4 * b]).then_inc(sem["qw%d" % h], 1)
     g.vector.wait_ge(sem.lx, 16)
     g.vector.quantize_mx(T.xq[:], T.xs[:], T.xt[:]).then_inc(sem.qx, 1)
     g.vector.wait_ge(sem.lr, 16)
     g.vector.quantize_mx(T.rq[:], T.rs[:], T.rtt[:]).then_inc(sem.qr, 1)
 
-    mask, ids = None, []
-    for r in peers:
-        d = T.cores[r]
+    mask, ids = None, {}
+    for k in range(1, N):
+        d = T.cores[(me + k) % N]
         one = topo.mask(core, d)
         mask = one if mask is None else mask & one
         rid, pid = topo.addr(d, core)
-        ids.append(DstId(rid=rid, pnc=pid))
-    engines = bin(mask).count("1")
-    arr = sem["arr%d" % me]
-    g.wait_ge(sem.qw, 1)
-    for view in (lambda: ws[:], lambda: wq[:].bitcast(dt.uint8)):
-        g.remote_dma_fused([RemoteDMATransfer(dst_ids=ids, dma_engine_mask=mask, remote_sem=arr,
-                                              srcs=[view()], dsts=[view() for _ in peers])], local_sem=sem.sent)
-    g.wait_ge(sem.sent, 2 * engines)
+        ids[k] = DstId(rid=rid, pnc=pid)
+    engines = count(mask)
+
+    def send(view, to, name):
+        g.remote_dma_fused([RemoteDMATransfer(dst_ids=[ids[k] for k in to], dma_engine_mask=mask,
+                                              remote_sem=sem["arr%d%s" % (me, name)],
+                                              srcs=[view()], dsts=[view() for _ in to])], local_sem=sem.sent)
+
+    first = lambda: wq[:, 0:H].bitcast(dt.uint8)
+    g.wait_ge(sem.qw0, 1)
+    send(first, (1, 3), "first")
+    inside = topo.mask(core, helpers[me]) & ~topo.mask(core, T.cores[(me + 2) % N])
+    rid, pid = topo.addr(helpers[me], core)
+    g.remote_dma(first(), first(), sem.relay, sem.sent, pid, rid, inside)
+    g.wait_ge(sem.qw1, 1)
+    send(lambda: ws[:], (1, 2, 3), "first")
+    send(lambda: wq[:, H:NC].bitcast(dt.uint8), (1, 2, 3), "second")
+    g.wait_ge(sem.sent, 3 * engines + count(inside))
 
     g.tensor.wait_ge(sem.qx, 1)
     g.tensor.wait_ge(sem.qr, 1)
     g.tensor.matmul_mx(T.plog[:, 0:128], T.xq[:], T.xs[:], T.rq[:], T.rs[:], True, True).then_inc(sem.plog, 1)
-    g.tensor.wait_ge(sem.qw, 1)
+    g.tensor.wait_ge(sem.qw0, 1)
+    g.tensor.wait_ge(sem.qw1, 1)
     g.tensor.matmul_mx(T.pown[:, 0:NC], T.xq[:], T.xs[:], wq[:], ws[:], True, True).then_inc(sem.pown, 1)
-    for k, e in enumerate(froms, 1):
-        g.tensor.wait_ge(sem["arr%d" % e], 2 * engines)
-        for h in range(2):
-            a, b = h * H, h * H + H
-            g.tensor.matmul_mx(T["p%d%d" % (k, h)][:, 0:H], T.xq[:], T.xs[:], T["wq%d" % e][:, a:b], T["ws%d" % e][:, a:b],
-                               True, True).then_inc(sem["p%d%d" % (k, h)], 1)
+    for k, h in TAIL:
+        e, (a, b) = (me - k) % N, halves[h]
+        if k == 2 and h == 0:
+            g.tensor.wait_ge(sem["arr%drelayed" % e], count(topo.mask(helpers[e], core)))
+        elif k == 2:
+            g.tensor.wait_ge(sem["arr%dfirst" % e], engines)
+            g.tensor.wait_ge(sem["arr%dsecond" % e], engines)
+        elif h == 0:
+            g.tensor.wait_ge(sem["arr%dfirst" % e], 2 * engines)
+        else:
+            g.tensor.wait_ge(sem["arr%dsecond" % e], engines)
+        g.tensor.matmul_mx(T["p%d%d" % (k, h)][:, 0:H], T.xq[:], T.xs[:], T["wq%d" % e][:, a:b], T["ws%d" % e][:, a:b],
+                           True, True).then_inc(sem["p%d%d" % (k, h)], 1)
 
     V = g.vector
     n = [0]
@@ -103,25 +149,25 @@ def rank_program(g, core, T, topo):
     S = g.scalar
     S.wait_ge(sem.gate, 1)
     S.wait_ge(sem.pown, 1)
-    S.activation(T.s0[:], T.pown[:, 0:NC], ActivationFunctionType.Copy, scale=T.gate[:, me:me + 1]).then_inc(sem.s00, 1)
-    for k, e in enumerate(froms, 1):
-        for h in range(2):
-            a, b = h * H, h * H + H
-            S.wait_ge(sem["p%d%d" % (k, h)], 1)
-            S.activation(T["s%d" % k][:, a:b], T["p%d%d" % (k, h)][:, 0:H], ActivationFunctionType.Copy,
-                         scale=T.gate[:, e:e + 1]).then_inc(sem["s%d%d" % (k, h)], 1)
+    S.activation(T.s0[:], T.pown[:, 0:NC], ActivationFunctionType.Copy, scale=T.gate[:, me:me + 1]).then_inc(sem.sown, 1)
+    for k, h in TAIL:
+        e, (a, b) = (me - k) % N, halves[h]
+        S.wait_ge(sem["p%d%d" % (k, h)], 1)
+        S.activation(T["s%d" % k][:, a:b], T["p%d%d" % (k, h)][:, 0:H], ActivationFunctionType.Copy,
+                     scale=T.gate[:, e:e + 1]).then_inc(sem["s%d%d" % (k, h)], 1)
 
-    V.wait_ge(sem.s00, 1)
-    for k in range(1, N):
-        prev = T.s0 if k == 1 else T["acc%d" % (k - 1)]
-        for h in range(2):
-            a, b = h * H, h * H + H
-            V.wait_ge(sem["s%d%d" % (k, h)], 1)
-            if k > 1:
-                V.wait_ge(sem["p0%d" % h], k - 1)
-            V.tensor_tensor(T["acc%d" % k][:, a:b], prev[:, a:b], T["s%d" % k][:, a:b], AluOpType.add).then_inc(sem["p0%d" % h], 1)
+    V.wait_ge(sem.sown, 1)
+    done = [0, 0]
+    for k, h in TAIL:
+        a, b = halves[h]
+        prev = T["acc%d" % done[h]] if done[h] else T.s0
+        V.wait_ge(sem["s%d%d" % (k, h)], 1)
+        if done[h]:
+            V.wait_ge(sem["acc%d" % h], done[h])
+        done[h] += 1
+        V.tensor_tensor(T["acc%d" % done[h]][:, a:b], prev[:, a:b], T["s%d" % k][:, a:b], AluOpType.add).then_inc(sem["acc%d" % h], 1)
 
-    g.sync.wait_ge(sem.p00, N - 1)
-    g.sync.wait_ge(sem.p01, N - 1)
-    g.sync.dma_start(T.y[:], T["acc%d" % (N - 1)][:]).then_inc(sem.stored, 16)
-    g.sync.wait_ge(sem.stored, 16)
+    for h, (a, b) in enumerate(halves):
+        g.sync.wait_ge(sem["acc%d" % h], N - 1)
+        g.sync.dma_start(T.y[:, a:b], T["acc%d" % (N - 1)][:, a:b]).then_inc(sem.stored, 16)
+    g.sync.wait_ge(sem.stored, 32)

from concourse.bass import DstId, RemoteDMATransfer
from concourse.mybir import dt, AluOpType, AxisListType, ActivationFunctionType

N = 4
NC = 256
H = NC // 2
BIG = -1e29

TAIL = [(1, 0), (3, 0), (1, 1), (2, 1), (2, 0), (3, 1)]

SCRATCH = {
    "wt": ("sbuf", [128, 4 * NC], "bfloat16"),
    "xt": ("sbuf", [128, 512], "bfloat16"),
    "rtt": ("sbuf", [128, 512], "bfloat16"),
    "xq": ("sbuf", [128, 128], "float8_e4m3fn_x4"),
    "xs": ("sbuf", [128, 128], "uint8"),
    "rq": ("sbuf", [128, 128], "float8_e4m3fn_x4"),
    "rs": ("sbuf", [128, 128], "uint8"),
    "m": ("sbuf", [128, 4], "float32"),
    "pen": ("sbuf", [128, 4], "float32"),
    "low": ("sbuf", [128, 4], "float32"),
    "m2": ("sbuf", [128, 4], "float32"),
    "take": ("sbuf", [128, 4], "float32"),
    "gate": ("sbuf", [128, 4], "float32"),
    "plog": ("psum", [128, 512], "float32"),
    "pown": ("psum", [128, 512], "float32"),
}
SEMAPHORES = ["lw0", "lw1", "lx", "lr", "qw0", "qw1", "qx", "qr", "plog", "pown", "v", "gate", "sent", "stored", "sown", "relay",
              "acc0", "acc1"]
for _e in range(N):
    SCRATCH["wq%d" % _e] = ("sbuf", [128, NC], "float8_e4m3fn_x4")
    SCRATCH["ws%d" % _e] = ("sbuf", [128, NC], "uint8")
    SCRATCH["s%d" % _e] = ("sbuf", [128, NC], "float32")
    SCRATCH["acc%d" % _e] = ("sbuf", [128, NC], "float32")
    SEMAPHORES += ["arr%d%s" % (_e, _p) for _p in ("first", "second", "relayed")]
    for _h in range(2):
        if _e:
            SCRATCH["p%d%d" % (_e, _h)] = ("psum", [128, 512], "float32")
            SEMAPHORES += ["p%d%d" % (_e, _h), "s%d%d" % (_e, _h)]


def count(mask):
    return bin(mask).count("1")


def helper_of(cores, r, topo):
    a, d, c = cores[r], cores[(r + 2) % N], 0
    while not (topo.host(c) == topo.host(a) and topo.chip(c) == topo.chip(a) and topo.die(c) != topo.die(a) and topo.may_write(c, d)):
        c += 1
    return c


def relay_program(g, core, T, topo, r):
    a, d = T.cores[r], T.cores[(r + 2) % N]
    piece = lambda: T["wq%d" % r][:, 0:H].bitcast(dt.uint8)
    mask = topo.mask(core, d)
    rid, pid = topo.addr(d, core)
    g.wait_ge(T.sem.relay, count(topo.mask(a, core) & ~topo.mask(a, d)))
    g.remote_dma(piece(), piece(), T.sem["arr%drelayed" % r], T.sem.sent, pid, rid, mask)
    g.wait_ge(T.sem.sent, count(mask))


def rank_program(g, core, T, topo):
    me = T.rank_of(core)
    helpers = [helper_of(T.cores, r, topo) for r in range(N)]
    if me is None:
        if core in helpers:
            relay_program(g, core, T, topo, helpers.index(core))
        return
    sem = T.sem
    halves = [(0, H), (H, NC)]

    for h, (a, b) in enumerate(halves):
        g.sync.dma_start(T.wt[:, 4 * a:4 * b], T.w[:, 4 * a:4 * b]).then_inc(sem["lw%d" % h], 16)
    g.sync.dma_start(T.xt[:], T.x[:]).then_inc(sem.lx, 16)
    g.sync.dma_start(T.rtt[:], T.rt[:]).then_inc(sem.lr, 16)

    wq, ws = T["wq%d" % me], T["ws%d" % me]
    for h, (a, b) in enumerate(halves):
        g.vector.wait_ge(sem["lw%d" % h], 16)
        g.vector.quantize_mx(wq[:, a:b], ws[:, a:b], T.wt[:, 4 * a:4 * b]).then_inc(sem["qw%d" % h], 1)
    g.vector.wait_ge(sem.lx, 16)
    g.vector.quantize_mx(T.xq[:], T.xs[:], T.xt[:]).then_inc(sem.qx, 1)
    g.vector.wait_ge(sem.lr, 16)
    g.vector.quantize_mx(T.rq[:], T.rs[:], T.rtt[:]).then_inc(sem.qr, 1)

    mask, ids = None, {}
    for k in range(1, N):
        d = T.cores[(me + k) % N]
        one = topo.mask(core, d)
        mask = one if mask is None else mask & one
        rid, pid = topo.addr(d, core)
        ids[k] = DstId(rid=rid, pnc=pid)
    engines = count(mask)

    def send(view, to, name):
        g.remote_dma_fused([RemoteDMATransfer(dst_ids=[ids[k] for k in to], dma_engine_mask=mask,
                                              remote_sem=sem["arr%d%s" % (me, name)],
                                              srcs=[view()], dsts=[view() for _ in to])], local_sem=sem.sent)

    first = lambda: wq[:, 0:H].bitcast(dt.uint8)
    g.wait_ge(sem.qw0, 1)
    send(first, (1, 3), "first")
    inside = topo.mask(core, helpers[me]) & ~topo.mask(core, T.cores[(me + 2) % N])
    rid, pid = topo.addr(helpers[me], core)
    g.remote_dma(first(), first(), sem.relay, sem.sent, pid, rid, inside)
    g.wait_ge(sem.qw1, 1)
    send(lambda: ws[:], (1, 2, 3), "first")
    send(lambda: wq[:, H:NC].bitcast(dt.uint8), (1, 2, 3), "second")
    g.wait_ge(sem.sent, 3 * engines + count(inside))

    g.tensor.wait_ge(sem.qx, 1)
    g.tensor.wait_ge(sem.qr, 1)
    g.tensor.matmul_mx(T.plog[:, 0:128], T.xq[:], T.xs[:], T.rq[:], T.rs[:], True, True).then_inc(sem.plog, 1)
    g.tensor.wait_ge(sem.qw0, 1)
    g.tensor.wait_ge(sem.qw1, 1)
    g.tensor.matmul_mx(T.pown[:, 0:NC], T.xq[:], T.xs[:], wq[:], ws[:], True, True).then_inc(sem.pown, 1)
    for k, h in TAIL:
        e, (a, b) = (me - k) % N, halves[h]
        if k == 2 and h == 0:
            g.tensor.wait_ge(sem["arr%drelayed" % e], count(topo.mask(helpers[e], core)))
        elif k == 2:
            g.tensor.wait_ge(sem["arr%dfirst" % e], engines)
            g.tensor.wait_ge(sem["arr%dsecond" % e], engines)
        elif h == 0:
            g.tensor.wait_ge(sem["arr%dfirst" % e], 2 * engines)
        else:
            g.tensor.wait_ge(sem["arr%dsecond" % e], engines)
        g.tensor.matmul_mx(T["p%d%d" % (k, h)][:, 0:H], T.xq[:], T.xs[:], T["wq%d" % e][:, a:b], T["ws%d" % e][:, a:b],
                           True, True).then_inc(sem["p%d%d" % (k, h)], 1)

    V = g.vector
    n = [0]

    def step(call):
        call.then_inc(sem.v, 1)
        n[0] += 1
        V.wait_ge(sem.v, n[0])

    L = T.plog[:, 0:N]
    V.wait_ge(sem.plog, 1)
    step(V.tensor_reduce(T.m[:, 0:1], L, AxisListType.X, AluOpType.max))
    step(V.tensor_scalar(T.pen[:], L, T.m[:, 0:1], BIG, AluOpType.is_ge, AluOpType.mult))
    step(V.tensor_tensor(T.low[:], L, T.pen[:], AluOpType.add))
    step(V.tensor_reduce(T.m2[:, 0:1], T.low[:], AxisListType.X, AluOpType.max))
    step(V.tensor_scalar(T.take[:], L, T.m2[:, 0:1], None, AluOpType.is_ge))
    V.tensor_tensor(T.gate[:], L, T.take[:], AluOpType.mult).then_inc(sem.gate, 1)

    S = g.scalar
    S.wait_ge(sem.gate, 1)
    S.wait_ge(sem.pown, 1)
    S.activation(T.s0[:], T.pown[:, 0:NC], ActivationFunctionType.Copy, scale=T.gate[:, me:me + 1]).then_inc(sem.sown, 1)
    for k, h in TAIL:
        e, (a, b) = (me - k) % N, halves[h]
        S.wait_ge(sem["p%d%d" % (k, h)], 1)
        S.activation(T["s%d" % k][:, a:b], T["p%d%d" % (k, h)][:, 0:H], ActivationFunctionType.Copy,
                     scale=T.gate[:, e:e + 1]).then_inc(sem["s%d%d" % (k, h)], 1)

    V.wait_ge(sem.sown, 1)
    done = [0, 0]
    for k, h in TAIL:
        a, b = halves[h]
        prev = T["acc%d" % done[h]] if done[h] else T.s0
        V.wait_ge(sem["s%d%d" % (k, h)], 1)
        if done[h]:
            V.wait_ge(sem["acc%d" % h], done[h])
        done[h] += 1
        V.tensor_tensor(T["acc%d" % done[h]][:, a:b], prev[:, a:b], T["s%d" % k][:, a:b], AluOpType.add).then_inc(sem["acc%d" % h], 1)

    for h, (a, b) in enumerate(halves):
        g.sync.wait_ge(sem["acc%d" % h], N - 1)
        g.sync.dma_start(T.y[:, a:b], T["acc%d" % (N - 1)][:, a:b]).then_inc(sem.stored, 16)
    g.sync.wait_ge(sem.stored, 32)
